import numpy as np
import ml_dtypes

BF16 = ml_dtypes.bfloat16


def bf(x):
    return np.asarray(x, np.float32).astype(BF16)


def f32(x):
    return np.asarray(x, np.float32)


def f64(x):
    return np.asarray(x).astype(np.float64)


def striped(idx):
    return np.tile(idx.reshape(-1, 16).T, (8, 1))


def rows(idx, k):
    return np.tile(idx, (k, 1))


def look(tab, idx):
    return np.take_along_axis(f64(tab), rows(idx, len(tab)), axis=1)


K, S, V, N = 512, 2048, 512, 512


def setup_inputs():
    return {"tab": f32(np.random.standard_normal((2, K, S))), "y": f32(np.random.standard_normal((K, V))), "offs": striped(np.random.permutation(S)[:N])}


def reference(tab, y, offs):
    idx = offs[:16].T.reshape(-1)
    x = (np.minimum(look(tab[0], idx), f64(y))) * (np.maximum(look(tab[1], idx), 0.0))
    return x

@@ -1,0 +1,38 @@
+import concourse.mybir as mybir
+
+F32, U16 = mybir.dt.float32, mybir.dt.uint16
+MIN, MULT = mybir.AluOpType.min, mybir.AluOpType.mult
+RELU = mybir.ActivationFunctionType.Relu
+P = 128
+
+
+def tile_lookup_vg_minrelu_out_kernel(tc, tab, y, offs, out):
+    nc = tc.nc
+    rows, entries = y.shape
+    places = tab.shape[2]
+    blocks = rows // P
+    with tc.tile_pool(name="held", bufs=1) as held:
+        offsets = held.tile([P, entries // 16], U16, name="offsets")
+        nc.sync.dma_start(offsets[:], offs)
+
+        gates, values, streams = [], [], []
+        for b in range(blocks):
+            block = slice(b * P, (b + 1) * P)
+            gate = held.tile([P, places], F32, name=f"gate{b}")
+            nc.sync.dma_start(gate[:], tab[1, block, :])
+            stream = held.tile([P, entries], F32, name=f"stream{b}")
+            nc.sync.dma_start(stream[:], y[block, :])
+            value = held.tile([P, places], F32, name=f"value{b}")
+            nc.sync.dma_start(value[:], tab[0, block, :])
+            gates.append(gate)
+            values.append(value)
+            streams.append(stream)
+
+        for b in range(blocks):
+            opened = held.tile([P, entries], F32, name=f"opened{b}")
+            nc.scalar.activation(opened[:], gates[b][:].indirect(offsets[:]), RELU)
+            capped = held.tile([P, entries], F32, name=f"capped{b}")
+            nc.vector.tensor_tensor(capped[:], values[b][:].indirect(offsets[:]), streams[b][:], MIN)
+            product = held.tile([P, entries], F32, name=f"product{b}")
+            nc.vector.tensor_tensor(product[:], capped[:], opened[:], MULT)
+            nc.sync.dma_start(out[b * P : (b + 1) * P, :], product[:])

@@ -11,28 +11,31 @@ def tile_lookup_vg_minrelu_out_kernel(tc, tab, y, offs, out):
     rows, entries = y.shape
     places = tab.shape[2]
     blocks = rows // P
+    tab_rows = tab.rearrange("t (p b) s -> t p b s", b=blocks)
+    y_rows = y.rearrange("(p b) j -> p (b j)", b=blocks)
+    out_rows = out.rearrange("(p b) j -> p b j", b=blocks)
     with tc.tile_pool(name="held", bufs=1) as held:
         offsets = held.tile([P, entries // 16], U16, name="offsets")
         nc.sync.dma_start(offsets[:], offs)
 
-        gates, values, streams = [], [], []
+        stream = held.tile([P, blocks * entries], F32, name="stream")
+        nc.sync.dma_start(stream[:], y_rows)
+        gates, values = [], []
         for b in range(blocks):
-            block = slice(b * P, (b + 1) * P)
             gate = held.tile([P, places], F32, name=f"gate{b}")
-            nc.sync.dma_start(gate[:], tab[1, block, :])
-            stream = held.tile([P, entries], F32, name=f"stream{b}")
-            nc.sync.dma_start(stream[:], y[block, :])
+            nc.sync.dma_start(gate[:], tab_rows[1, :, b, :])
             value = held.tile([P, places], F32, name=f"value{b}")
-            nc.sync.dma_start(value[:], tab[0, block, :])
+            nc.sync.dma_start(value[:], tab_rows[0, :, b, :])
             gates.append(gate)
             values.append(value)
-            streams.append(stream)
 
         for b in range(blocks):
             opened = held.tile([P, entries], F32, name=f"opened{b}")
             nc.scalar.activation(opened[:], gates[b][:].indirect(offsets[:]), RELU)
             capped = held.tile([P, entries], F32, name=f"capped{b}")
-            nc.vector.tensor_tensor(capped[:], values[b][:].indirect(offsets[:]), streams[b][:], MIN)
+            nc.vector.tensor_tensor(
+                capped[:], values[b][:].indirect(offsets[:]), stream[:, b * entries : (b + 1) * entries], MIN
+            )
             product = held.tile([P, entries], F32, name=f"product{b}")
             nc.vector.tensor_tensor(product[:], capped[:], opened[:], MULT)
-            nc.sync.dma_start(out[b * P : (b + 1) * P, :], product[:])
+            nc.sync.dma_start(out_rows[:, b, :], product[:])

@@ -20,22 +20,27 @@ def tile_lookup_vg_minrelu_out_kernel(tc, tab, y, offs, out):
 
         stream = held.tile([P, blocks * entries], F32, name="stream")
         nc.sync.dma_start(stream[:], y_rows)
-        gates, values = [], []
+        values, gates = [], []
         for b in range(blocks):
-            gate = held.tile([P, places], F32, name=f"gate{b}")
-            nc.sync.dma_start(gate[:], tab_rows[1, :, b, :])
             value = held.tile([P, places], F32, name=f"value{b}")
             nc.sync.dma_start(value[:], tab_rows[0, :, b, :])
-            gates.append(gate)
+            gate = held.tile([P, places], F32, name=f"gate{b}")
+            nc.sync.dma_start(gate[:], tab_rows[1, :, b, :])
             values.append(value)
+            gates.append(gate)
 
         for b in range(blocks):
-            opened = held.tile([P, entries], F32, name=f"opened{b}")
-            nc.scalar.activation(opened[:], gates[b][:].indirect(offsets[:]), RELU)
+            pieces = 2 if b == blocks - 1 else 1
+            width = entries // pieces
             capped = held.tile([P, entries], F32, name=f"capped{b}")
             nc.vector.tensor_tensor(
                 capped[:], values[b][:].indirect(offsets[:]), stream[:, b * entries : (b + 1) * entries], MIN
             )
-            product = held.tile([P, entries], F32, name=f"product{b}")
-            nc.vector.tensor_tensor(product[:], capped[:], opened[:], MULT)
-            nc.sync.dma_start(out_rows[:, b, :], product[:])
+            for i in range(pieces):
+                piece = slice(i * width, (i + 1) * width)
+                listed = offsets[:, i * width // 16 : (i + 1) * width // 16]
+                opened = held.tile([P, width], F32, name=f"opened{b}_{i}")
+                nc.scalar.activation(opened[:], gates[b][:].indirect(listed), RELU)
+                product = held.tile([P, width], F32, name=f"product{b}_{i}")
+                nc.vector.tensor_tensor(product[:], capped[:, piece], opened[:], MULT)
+                nc.sync.dma_start(out_rows[:, b, piece], product[:])

@@ -23,7 +23,7 @@ def tile_lookup_vg_minrelu_out_kernel(tc, tab, y, offs, out):
         values, gates = [], []
         for b in range(blocks):
             value = held.tile([P, places], F32, name=f"value{b}")
-            nc.sync.dma_start(value[:], tab_rows[0, :, b, :])
+            nc.scalar.dma_start(value[:], tab_rows[0, :, b, :])
             gate = held.tile([P, places], F32, name=f"gate{b}")
             nc.sync.dma_start(gate[:], tab_rows[1, :, b, :])
             values.append(value)

import concourse.mybir as mybir

F32, U16 = mybir.dt.float32, mybir.dt.uint16
MIN, MULT = mybir.AluOpType.min, mybir.AluOpType.mult
RELU = mybir.ActivationFunctionType.Relu
P = 128


def tile_lookup_vg_minrelu_out_kernel(tc, tab, y, offs, out):
    nc = tc.nc
    rows, entries = y.shape
    places = tab.shape[2]
    blocks = rows // P
    tab_rows = tab.rearrange("t (p b) s -> t p b s", b=blocks)
    y_rows = y.rearrange("(p b) j -> p (b j)", b=blocks)
    out_rows = out.rearrange("(p b) j -> p b j", b=blocks)
    with tc.tile_pool(name="held", bufs=1) as held:
        offsets = held.tile([P, entries // 16], U16, name="offsets")
        nc.sync.dma_start(offsets[:], offs)

        stream = held.tile([P, blocks * entries], F32, name="stream")
        nc.sync.dma_start(stream[:], y_rows)
        values, gates = [], []
        for b in range(blocks):
            value = held.tile([P, places], F32, name=f"value{b}")
            nc.scalar.dma_start(value[:], tab_rows[0, :, b, :])
            gate = held.tile([P, places], F32, name=f"gate{b}")
            nc.sync.dma_start(gate[:], tab_rows[1, :, b, :])
            values.append(value)
            gates.append(gate)

        for b in range(blocks):
            pieces = 2 if b == blocks - 1 else 1
            width = entries // pieces
            capped = held.tile([P, entries], F32, name=f"capped{b}")
            nc.vector.tensor_tensor(
                capped[:], values[b][:].indirect(offsets[:]), stream[:, b * entries : (b + 1) * entries], MIN
            )
            for i in range(pieces):
                piece = slice(i * width, (i + 1) * width)
                listed = offsets[:, i * width // 16 : (i + 1) * width // 16]
                opened = held.tile([P, width], F32, name=f"opened{b}_{i}")
                nc.scalar.activation(opened[:], gates[b][:].indirect(listed), RELU)
                product = held.tile([P, width], F32, name=f"product{b}_{i}")
                nc.vector.tensor_tensor(product[:], capped[:, piece], opened[:], MULT)
                nc.sync.dma_start(out_rows[:, b, piece], product[:])
